import numpy as np
import ml_dtypes


def mxq(x, axis, fmt="e4m3"):
    dtype, down = {"e4m3": (ml_dtypes.float8_e4m3fn, 7), "e5m2": (ml_dtypes.float8_e5m2, 14)}[fmt]
    v = np.moveaxis(np.asarray(x, np.float32).astype(ml_dtypes.bfloat16).astype(np.float64), axis, -1)
    blocks = v.reshape(v.shape[:-1] + (-1, 32))
    amax = np.abs(blocks).max(-1, keepdims=True)
    byte = np.maximum(np.where(amax > 0, np.frexp(amax)[1] - 1 + 127, 0) - down, 1)
    scale = np.exp2(byte - 127.0)
    codes = (blocks / scale).astype(np.float32).astype(dtype).astype(np.float64)
    return np.moveaxis((codes * scale).reshape(v.shape), -1, axis)


WIDE = False


def mx_kscale(k):
    if not WIDE:
        return np.ones(k)
    levels = np.array([10, -10, 5, -5, 0])
    if k % 512:
        return np.exp2(np.random.permutation(np.resize(levels, k // 32))).repeat(32)
    a = np.empty((k // 512, 16))
    for p in range(k // 512):
        a[p, :8] = np.random.permutation(np.resize(levels, 8))
        for g in range(8):
            far = levels[np.abs(levels - a[p, g]) >= 10]
            a[p, g + 8] = far[np.random.randint(len(far))]
    return np.exp2(a.ravel()).repeat(32)


def f64(x):
    return np.asarray(x).astype(np.float64)


def striped(idx):
    return np.tile(idx.reshape(-1, 16).T, (8, 1)).astype(np.uint16)


def unstriped(offs):
    return offs[:16].T.reshape(-1).astype(np.int64)


E2M1 = np.array([0.0, 0.5, 1.0, 1.5, 2.0, 3.0, 4.0, 6.0, -0.0, -0.5, -1.0, -1.5, -2.0, -3.0, -4.0, -6.0])


def pack_weight(w, fmt):
    k, n = w.shape
    w = f64(np.asarray(w, np.float32).astype(ml_dtypes.bfloat16)).reshape(k // 32, 32, n)
    amax = np.abs(w).max(1)
    if fmt == "e4m3":
        byte = np.frexp(amax)[1] - 1 + 127 - 7
    else:
        mant, ex = np.frexp(amax / 6.0)
        byte = np.where(mant > 0.5, ex, ex - 1) + 127
    byte = np.clip(np.where(amax > 0, byte, 1), 1, 254)
    scaled = (w * np.exp2(127.0 - byte)[:, None, :]).reshape(k, n).astype(np.float32)
    by_word = np.ascontiguousarray(scaled.reshape(k // 512, 128, 4, n).transpose(0, 1, 3, 2))
    if fmt == "e4m3":
        words = by_word.astype(ml_dtypes.float8_e4m3fn).view(np.uint8)
    else:
        c = by_word.astype(ml_dtypes.float4_e2m1fn).view(np.uint8) & 0xF
        words = (c[..., 0::2] | (c[..., 1::2] << 4)).reshape(k // 512, 128, 2 * n)
    return np.ascontiguousarray(words), np.ascontiguousarray(byte.astype(np.uint8).reshape(k // 512, 16, n))


def unpack_weight(words, scales, fmt):
    g, _, n = scales.shape
    words = np.ascontiguousarray(words).reshape(g, 128, n, -1)
    if fmt == "e4m3":
        vals = words.view(ml_dtypes.float8_e4m3fn).astype(np.float64)
    else:
        nib = np.empty((g, 128, n, 4), np.uint8)
        nib[..., 0::2] = words & 0xF
        nib[..., 1::2] = words >> 4
        vals = E2M1[nib]
    vals = vals * np.repeat(np.exp2(scales.astype(np.float64) - 127.0), 8, axis=1)[..., None]
    return vals.transpose(0, 1, 3, 2).reshape(g * 512, n)


def gelu(v):
    return 0.5 * v * (1.0 + np.tanh(np.sqrt(2.0 / np.pi) * (v + 0.044715 * v**3)))


K, T, S, P, H, N = 1536, 2048, 1024, 512, 1024, 768

def setup_inputs():
    n = np.random.standard_normal
    s = mx_kscale(K)[:, None]
    u = mx_kscale(H)[:, None]
    tab_words, tab_scales = pack_weight(n((K, T)) * s, "e4m3")
    w1 = (0.95 * n((K, H)) / np.sqrt(K) / s).astype(np.float32)
    w4_words, w4_scales = pack_weight(n((H, N)) / np.sqrt(H) / u, "e2m1")
    wc = (0.6 * n((H, N)) / np.sqrt(H) / u).astype(np.float32)
    return {
        "tab_words": tab_words, "tab_scales": tab_scales,
        "offs": striped(np.random.permutation(T)[:S]),
        "pos1": striped(np.random.permutation(S)[:P]),
        "pos2": striped(np.random.permutation(S)[:P]),
        "w1": w1,
        "comfort": n(H).astype(np.float32),
        "reach": np.random.uniform(-2.0, 4.0, H).astype(np.float32),
        "pairw": (n((H, P)) * u).astype(np.float32),
        "gain": (np.random.uniform(0.6, 1.6, H) * u[:, 0]).astype(np.float32),
        "w4_words": w4_words, "w4_scales": w4_scales,
        "wc": wc,
    }

def reference(tab_words, tab_scales, offs, pos1, pos2, w1, comfort, reach, pairw, gain, w4_words, w4_scales, wc):
    v = unpack_weight(tab_words, tab_scales, "e4m3")[:, unstriped(offs)]
    h = mxq(f64(w1), 0, "e4m3").T @ v
    a = 1.0 / (1.0 + np.exp(-(h[:, unstriped(pos1)] + f64(comfort)[:, None])))
    c = h[:, unstriped(pos2)]
    both = np.maximum(c, f64(reach)[:, None] * a) * f64(pairw)
    own = f64(gain)[:, None] * c
    qb = mxq(both, 0, "e4m3")
    qo = mxq(own, 0, "e4m3")
    w4 = unpack_weight(w4_words, w4_scales, "e2m1")
    out = w4.T @ qb + mxq(f64(wc), 0, "e4m3").T @ qo
    return out

@@ -1,0 +1,340 @@
+from contextlib import ExitStack
+
+import concourse.mybir as mybir
+
+K, T, S, M, H, N = 1536, 2048, 1024, 512, 1024, 768
+FLOPS = 2 * K * H * S + 2 * 2 * H * N * M
+
+F32 = mybir.dt.float32
+BF16 = mybir.dt.bfloat16
+I32 = mybir.dt.int32
+U32 = mybir.dt.uint32
+U16 = mybir.dt.uint16
+U8 = mybir.dt.uint8
+FP8X4 = mybir.dt.float8_e4m3fn_x4
+FP4X4 = mybir.dt.float4_e2m1fn_x4
+ALU = mybir.AluOpType
+ACT = mybir.ActivationFunctionType
+
+P = 128
+PACK = 4
+PASS = P * PACK
+BANK = 512
+K_PASSES = K // PASS
+H_PASSES = H // PASS
+N_HALF = N // 2
+M_HALF = M // 2
+WCB = 2
+PARTS = [(0, 256), (256, 128), (384, 128)]
+
+
+def tile_list_therapist_pairing_scores_kernel(
+    tc, tab_words, tab_scales, offs, pos1, pos2, w1, comfort, reach, pairw, gain, w4_words, w4_scales, wc, out
+):
+    nc = tc.nc
+    with ExitStack() as ctx:
+        keep = ctx.enter_context(tc.tile_pool(name="keep", bufs=1))
+        ring = ctx.enter_context(tc.tile_pool(name="ring", bufs=1))
+        psum = ctx.enter_context(tc.psum_pool(name="psum", bufs=1))
+
+        def copy_on(engine, dst, src):
+            if engine == "v":
+                nc.vector.tensor_copy(out=dst, in_=src)
+            else:
+                nc.scalar.copy(out=dst, in_=src)
+
+        offs_sb = keep.tile([P, S // 16], U16, name="offs_sb")
+        pos1_sb = keep.tile([P, M // 16], U16, name="pos1_sb")
+        pos2_sb = keep.tile([P, M // 16], U16, name="pos2_sb")
+        tab_sc = keep.tile([P, T], U8, name="tab_sc", align_bytes=64)
+        w4_sc = keep.tile([P, H_PASSES, N], U8, name="w4_sc", align_bytes=64)
+        nc.vector.memset(tab_sc[:].bitcast(I32), 0)
+        nc.vector.memset(w4_sc[:].rearrange("p a n -> p (a n)").bitcast(I32), 0)
+
+        tab_w = [keep.tile([P, T], I32, name=f"tab_w{a}") for a in range(K_PASSES)]
+
+        def load_tab(a):
+            nc.sync.dma_start(out=tab_w[a][:], in_=tab_words[a].rearrange("p t i -> p (t i)").bitcast(I32))
+
+        def load_rows(src, row0, col0, width, tag, bufs):
+            raw = ring.tile([P, PACK, width], F32, name=tag, tag=tag, bufs=bufs)
+            nc.sync.dma_start(
+                out=raw[:], in_=src[row0 : row0 + PASS, col0 : col0 + width].rearrange("(p j) c -> p j c", j=PACK)
+            )
+            return raw
+
+        def load_vec(src, name):
+            vec = keep.tile([P, H_PASSES * PACK], F32, name=name)
+            nc.sync.dma_start(
+                out=vec[:].rearrange("p (b t) -> p b t", t=PACK), in_=src.rearrange("(b p t) -> p b t", p=P, t=PACK)
+            )
+            return vec
+
+        w1_raw = {}
+        load_tab(0)
+        nc.sync.dma_start(offs_sb[:], offs)
+        w1_raw[0, 0] = [load_rows(w1, 0, 0, PASS, "raw", 5)]
+        tab_sc_i32 = tab_scales.bitcast(I32)
+        for q in range(4):
+            nc.sync.dma_start(
+                out=tab_sc[32 * q : 32 * q + 4 * K_PASSES, :].bitcast(I32), in_=tab_sc_i32[:, 4 * q : 4 * q + 4, :]
+            )
+        load_tab(1)
+        w1_raw[1, 0] = [load_rows(w1, PASS, 0, PASS, "raw", 5)]
+        load_tab(2)
+        w1_raw[2, 0] = [load_rows(w1, 2 * PASS, u * 256, 256, "raw_half", 2) for u in range(2)]
+        nc.sync.dma_start(pos2_sb[:], pos2)
+        nc.sync.dma_start(pos1_sb[:], pos1)
+        comfort_sb = load_vec(comfort, "comfort_sb")
+        reach_sb = load_vec(reach, "reach_sb")
+        gain_sb = load_vec(gain, "gain_sb")
+        w1_raw[0, 1] = [load_rows(w1, 0, PASS, PASS, "raw", 5)]
+        w1_raw[1, 1] = [load_rows(w1, PASS, PASS, PASS, "raw", 5)]
+        w1_raw[2, 1] = [load_rows(w1, 2 * PASS, PASS, PASS, "raw", 5)]
+        pw = {0: load_rows(pairw, 0, 0, M, "pw", 2)}
+        wc_raw = {}
+        for u in range(2):
+            wc_raw[0, u] = load_rows(wc, 0, u * N_HALF, N_HALF, "raw", 5)
+        w4 = keep.tile([P, H_PASSES, 2 * N], U8, name="w4", align_bytes=64)
+        nc.sync.dma_start(out=w4[:].bitcast(I32), in_=w4_words.bitcast(I32).rearrange("a p x -> p a x"))
+        w4_sc_i32 = w4_scales.bitcast(I32)
+        for q in range(4):
+            nc.sync.dma_start(
+                out=w4_sc[32 * q : 32 * q + 4, :, :].bitcast(I32),
+                in_=w4_sc_i32[:, 4 * q : 4 * q + 4, :].rearrange("a r n -> r a n"),
+            )
+        for u in range(2):
+            wc_raw[1, u] = load_rows(wc, PASS, u * N_HALF, N_HALF, "raw", 5)
+        pw[1] = load_rows(pairw, PASS, 0, M, "pw", 2)
+
+        got_sc = keep.tile([P, S], U8, name="got_sc", align_bytes=64)
+        got_w = [keep.tile([P, S], U32, name=f"got_w{a}", align_bytes=64) for a in range(K_PASSES)]
+
+        def gather_tab(a):
+            nc.vector.tensor_copy(out=got_w[a][:], in_=tab_w[a][:].bitcast(U32).indirect(offs_sb[:]))
+
+        w1_woven, w1_codes, w1_planes = {}, {}, {}
+
+        def weave_w1(a, b, tp, engine, piece=None):
+            if (a, b, tp) not in w1_woven:
+                w1_woven[a, b, tp] = ring.tile([P, 2, P, PACK], BF16, name="w1_woven", tag="w1_woven", bufs=4, align_bytes=64)
+            woven = w1_woven[a, b, tp]
+            raws = w1_raw[a, b]
+            nq = P // len(raws)
+            for u in range(len(raws)) if piece is None else [piece]:
+                src = raws[u][:].rearrange("p j (q t) -> p q j t", t=PACK)[:, :, :, 2 * tp : 2 * tp + 2]
+                dst = woven[:, :, u * nq : (u + 1) * nq, :].rearrange("p t q j -> p q j t")
+                copy_on(engine, dst, src)
+
+        def quant_w1(a, b, tp):
+            codes = keep.tile([P, 2 * P], U32, name=f"w1_codes{a}{b}{tp}", align_bytes=64)
+            plane = keep.tile([P, 2 * P], U8, name=f"w1_plane{a}{b}{tp}", align_bytes=64)
+            nc.vector.quantize_mx(
+                out=codes[:].bitcast(FP8X4), scales=plane[:], in_=w1_woven[a, b, tp][:].rearrange("p t q j -> p (t q j)")
+            )
+            w1_codes[a, b, tp], w1_planes[a, b, tp] = codes, plane
+
+        h_acc = {}
+
+        def stage1(a, b, t):
+            cols = slice((t % 2) * P, (t % 2 + 1) * P)
+            for u in range(2):
+                if a == 0:
+                    h_acc[b, t, u] = psum.tile([P, BANK], F32, name=f"bank{2 * t + u}", tag=f"bank{2 * t + u}")
+                tok = slice(u * BANK, (u + 1) * BANK)
+                nc.tensor.matmul_mx(
+                    out=h_acc[b, t, u][:],
+                    lhsT=w1_codes[a, b, t // 2][:, cols].bitcast(FP8X4),
+                    lhsT_scale=w1_planes[a, b, t // 2][:, cols],
+                    rhs=got_w[a][:, tok].bitcast(FP8X4),
+                    rhs_scale=got_sc[4 * a : P, tok],
+                    start=(a == 0),
+                    stop=(a == K_PASSES - 1),
+                )
+
+        h_sb, gate, own_c = {}, {}, {}
+
+        def evac_h(b, t, engines):
+            h_sb[b, t] = ring.tile([P, S], F32, name="h_sb", tag="h_sb", bufs=6)
+            for u in range(2):
+                copy_on(engines[u], h_sb[b, t][:, u * BANK : (u + 1) * BANK], h_acc[b, t, u][:])
+
+        def look(b, t):
+            if t == 0:
+                gate[b] = ring.tile([P, PACK, M], F32, name="gate", tag="gate", bufs=2)
+            col = slice(PACK * b + t, PACK * b + t + 1)
+            nc.scalar.activation(
+                out=gate[b][:, t, :], in_=h_sb[b, t][:].indirect(pos1_sb[:]), func=ACT.Sigmoid, bias=comfort_sb[:, col]
+            )
+
+        def pick(b, t):
+            if t == 0:
+                own_c[b] = ring.tile([P, PACK, M], F32, name="client", tag="client", bufs=1)
+            nc.vector.tensor_copy(out=own_c[b][:, t, :], in_=h_sb[b, t][:].indirect(pos2_sb[:]))
+
+        def larger(b, t):
+            col = slice(PACK * b + t, PACK * b + t + 1)
+            nc.vector.scalar_tensor_tensor(
+                out=gate[b][:, t, :], in0=gate[b][:, t, :], scalar=reach_sb[:, col], in1=own_c[b][:, t, :],
+                op0=ALU.mult, op1=ALU.max,
+            )
+
+        woven2, codes2, planes2 = {}, {}, {}
+
+        def pairs(ap):
+            return ap.rearrange("p t (c i) -> p c t i", i=2)
+
+        def weave2(kind, b, m0, width):
+            cols = slice(m0, m0 + width)
+            woven = ring.tile([P, width * PACK], BF16, name="woven2", tag="woven2", bufs=3, align_bytes=64)
+            dst = woven[:].rearrange("p (c i t) -> p c t i", i=2, t=PACK)
+            if kind == "own":
+                factor = gain_sb[:, PACK * b : PACK * (b + 1)].unsqueeze(1).unsqueeze(3).broadcast_to([P, width // 2, PACK, 2])
+                nc.vector.tensor_tensor(out=dst, in0=pairs(own_c[b][:, :, cols]), in1=factor, op=ALU.mult)
+            else:
+                nc.vector.tensor_tensor(out=dst, in0=pairs(gate[b][:, :, cols]), in1=pairs(pw[b][:, :, cols]), op=ALU.mult)
+            woven2[kind, b, m0] = woven
+
+        def quant2(kind, b, m0, width):
+            if (kind, b) not in codes2:
+                codes2[kind, b] = {}
+            codes = keep.tile([P, width], U32, name=f"{kind}_codes{b}{m0}", align_bytes=64)
+            plane = keep.tile([P, width], U8, name=f"{kind}_plane{b}{m0}", align_bytes=64)
+            nc.vector.quantize_mx(out=codes[:].bitcast(FP8X4), scales=plane[:], in_=woven2[kind, b, m0][:])
+            codes2[kind, b][m0] = (codes, plane, width)
+
+        wc_woven, wc_codes, wc_planes = {}, {}, {}
+
+        def weave_wc(b, u, engine):
+            woven = ring.tile([P, N_HALF * PACK], BF16, name="wc_woven", tag="wc_woven", bufs=WCB, align_bytes=64)
+            copy_on(engine, woven[:].rearrange("p (c i t) -> p c t i", i=2, t=PACK), pairs(wc_raw[b, u][:]))
+            wc_woven[b, u] = woven
+
+        def quant_wc(b, u):
+            codes = keep.tile([P, N_HALF], U32, name=f"wc_codes{b}{u}", align_bytes=64)
+            plane = keep.tile([P, N_HALF], U8, name=f"wc_plane{b}{u}", align_bytes=64)
+            nc.vector.quantize_mx(out=codes[:].bitcast(FP8X4), scales=plane[:], in_=wc_woven[b, u][:])
+            wc_codes[b, u], wc_planes[b, u] = codes, plane
+
+        out_acc, seen = {}, {}
+        part_banks = {}
+        first_bank = 0
+        for m0, width in PARTS:
+            per_bank = BANK // width
+            count = -(-6 // per_bank)
+            part_banks[m0] = (first_bank, per_bank, width)
+            first_bank += count
+
+        def stage2(kind, b, m0, tiles=range(6)):
+            bank0, per_bank, width = part_banks[m0]
+            src0 = max(x for x in codes2[kind, b] if x <= m0)
+            codes, plane, wide = codes2[kind, b][src0]
+            cols = slice(m0 - src0, m0 - src0 + width)
+            for nt in tiles:
+                bank, side = divmod(nt, per_bank)
+                held = min(per_bank, 6 - bank * per_bank)
+                if (m0, bank) not in out_acc:
+                    out_acc[m0, bank] = psum.tile([P, BANK], F32, name=f"bank{bank0 + bank}", tag=f"bank{bank0 + bank}")
+                    seen[m0, bank] = 0
+                if kind == "own":
+                    u, k = divmod(nt, 3)
+                    lhsT = wc_codes[b, u][:, k * P : (k + 1) * P].bitcast(FP8X4)
+                    lhsT_scale = wc_planes[b, u][:, k * P : (k + 1) * P]
+                else:
+                    lhsT = w4[:, b, 2 * nt * P : 2 * (nt + 1) * P].bitcast(FP4X4)
+                    lhsT_scale = w4_sc[:, b, nt * P : (nt + 1) * P]
+                seen[m0, bank] = seen[m0, bank] + 1
+                nc.tensor.matmul_mx(
+                    out=out_acc[m0, bank][:, side * width : (side + 1) * width],
+                    lhsT=lhsT, lhsT_scale=lhsT_scale,
+                    rhs=codes[:, cols].bitcast(FP8X4), rhs_scale=plane[:, cols],
+                    start=(seen[m0, bank] == 1), stop=(seen[m0, bank] == 4 * held),
+                )
+
+        def store(m0, engines):
+            bank0, per_bank, width = part_banks[m0]
+            for bank in range(-(-6 // per_bank)):
+                held = min(per_bank, 6 - bank * per_bank)
+                res = keep.tile([P, held * width], F32, name=f"res{m0}{bank}")
+                copy_on(engines[bank], res[:], out_acc[m0, bank][:, : held * width])
+                n0 = P * per_bank * bank
+                nc.sync.dma_start(
+                    out=out[n0 : n0 + held * P, m0 : m0 + width].rearrange("(k p) m -> p k m", p=P),
+                    in_=res[:].rearrange("p (k m) -> p k m", k=held),
+                )
+
+        def rows(b, t, engines):
+            evac_h(b, t, engines)
+            pick(b, t)
+            look(b, t)
+            larger(b, t)
+
+
+        gather_tab(0)
+        weave_w1(0, 0, 0, "s")
+        weave_w1(0, 0, 1, "s")
+        nc.vector.tensor_copy(out=got_sc[:], in_=tab_sc[:].indirect(offs_sb[:]))
+        quant_w1(0, 0, 0)
+        quant_w1(0, 0, 1)
+        for t in range(PACK):
+            stage1(0, 0, t)
+        gather_tab(1)
+        weave_w1(1, 0, 0, "s")
+        weave_w1(1, 0, 1, "v")
+        quant_w1(1, 0, 0)
+        quant_w1(1, 0, 1)
+        for t in range(PACK):
+            stage1(1, 0, t)
+        gather_tab(2)
+        weave_w1(2, 0, 0, "s", 0)
+        weave_w1(2, 0, 0, "v", 1)
+        quant_w1(2, 0, 0)
+        weave_w1(2, 0, 1, "s", 0)
+        weave_w1(2, 0, 1, "s", 1)
+        quant_w1(2, 0, 1)
+        for t in range(PACK):
+            stage1(2, 0, t)
+
+        def unit(a, tp, engine):
+            weave_w1(a, 1, tp, engine)
+            quant_w1(a, 1, tp)
+            for t in (2 * tp, 2 * tp + 1):
+                stage1(a, 1, t)
+
+        rows(0, 0, "sv")
+        unit(0, 0, "v")
+        rows(0, 1, "ss")
+        unit(1, 0, "v")
+        rows(0, 2, "ss")
+        unit(2, 0, "v")
+        rows(0, 3, "ss")
+        unit(0, 1, "s")
+        unit(1, 1, "s")
+        unit(2, 1, "s")
+        weave2("own", 0, 0, M)
+        weave2("both", 0, 0, M)
+        quant2("own", 0, 0, M)
+        quant2("both", 0, 0, M)
+        for t in range(PACK):
+            rows(1, t, "ss")
+        for m0, width in PARTS:
+            stage2("both", 0, m0)
+        for b in range(2):
+            for u in range(2):
+                weave_wc(b, u, "ssss"[2 * b + u])
+        quant_wc(0, 0)
+        quant_wc(0, 1)
+        for m0, width in PARTS:
+            stage2("own", 0, m0)
+        for k, (m0, width) in enumerate(PARTS):
+            weave2("own", 1, m0, width)
+            if k == 0:
+                quant_wc(1, 0)
+            weave2("both", 1, m0, width)
+            if k == 0:
+                quant_wc(1, 1)
+            quant2("own", 1, m0, width)
+            stage2("own", 1, m0)
+            quant2("both", 1, m0, width)
+            stage2("both", 1, m0)
+            store(m0, "sss" if k < len(PARTS) - 1 else "svs")

@@ -46,7 +46,7 @@ def tile_list_therapist_pairing_scores_kernel(
         offs_sb = keep.tile([P, S // 16], U16, name="offs_sb")
         pos1_sb = keep.tile([P, M // 16], U16, name="pos1_sb")
         pos2_sb = keep.tile([P, M // 16], U16, name="pos2_sb")
-        tab_sc = keep.tile([P, T], U8, name="tab_sc", align_bytes=64)
+        tab_sc = ring.tile([P, T], U8, name="tab_sc", tag="tab_sc", align_bytes=64)
         w4_sc = keep.tile([P, H_PASSES, N], U8, name="w4_sc", align_bytes=64)
         nc.vector.memset(tab_sc[:].bitcast(I32), 0)
         nc.vector.memset(w4_sc[:].rearrange("p a n -> p (a n)").bitcast(I32), 0)
@@ -56,9 +56,9 @@ def tile_list_therapist_pairing_scores_kernel(
         def load_tab(a):
             nc.sync.dma_start(out=tab_w[a][:], in_=tab_words[a].rearrange("p t i -> p (t i)").bitcast(I32))
 
-        def load_rows(src, row0, col0, width, tag, bufs):
+        def load_rows(src, row0, col0, width, tag, bufs, queue=nc.sync):
             raw = ring.tile([P, PACK, width], F32, name=tag, tag=tag, bufs=bufs)
-            nc.sync.dma_start(
+            queue.dma_start(
                 out=raw[:], in_=src[row0 : row0 + PASS, col0 : col0 + width].rearrange("(p j) c -> p j c", j=PACK)
             )
             return raw
@@ -85,16 +85,14 @@ def tile_list_therapist_pairing_scores_kernel(
         w1_raw[2, 0] = [load_rows(w1, 2 * PASS, u * 256, 256, "raw_half", 2) for u in range(2)]
         nc.sync.dma_start(pos2_sb[:], pos2)
         nc.sync.dma_start(pos1_sb[:], pos1)
+        pw, wc_raw = {}, {}
         comfort_sb = load_vec(comfort, "comfort_sb")
         reach_sb = load_vec(reach, "reach_sb")
-        gain_sb = load_vec(gain, "gain_sb")
         w1_raw[0, 1] = [load_rows(w1, 0, PASS, PASS, "raw", 5)]
         w1_raw[1, 1] = [load_rows(w1, PASS, PASS, PASS, "raw", 5)]
         w1_raw[2, 1] = [load_rows(w1, 2 * PASS, PASS, PASS, "raw", 5)]
-        pw = {0: load_rows(pairw, 0, 0, M, "pw", 2)}
-        wc_raw = {}
-        for u in range(2):
-            wc_raw[0, u] = load_rows(wc, 0, u * N_HALF, N_HALF, "raw", 5)
+        gain_sb = load_vec(gain, "gain_sb")
+        pw[0] = load_rows(pairw, 0, 0, M, "pw", 2)
         w4 = keep.tile([P, H_PASSES, 2 * N], U8, name="w4", align_bytes=64)
         nc.sync.dma_start(out=w4[:].bitcast(I32), in_=w4_words.bitcast(I32).rearrange("a p x -> p a x"))
         w4_sc_i32 = w4_scales.bitcast(I32)
@@ -103,9 +101,11 @@ def tile_list_therapist_pairing_scores_kernel(
                 out=w4_sc[32 * q : 32 * q + 4, :, :].bitcast(I32),
                 in_=w4_sc_i32[:, 4 * q : 4 * q + 4, :].rearrange("a r n -> r a n"),
             )
-        for u in range(2):
-            wc_raw[1, u] = load_rows(wc, PASS, u * N_HALF, N_HALF, "raw", 5)
         pw[1] = load_rows(pairw, PASS, 0, M, "pw", 2)
+        wc_raw[0, 0] = load_rows(wc, 0, 0, N_HALF, "raw_half", 2, nc.scalar)
+        wc_raw[0, 1] = load_rows(wc, 0, N_HALF, N_HALF, "raw_half", 2, nc.scalar)
+        wc_raw[1, 0] = load_rows(wc, PASS, 0, N_HALF, "raw_half", 2, nc.scalar)
+        wc_raw[1, 1] = load_rows(wc, PASS, N_HALF, N_HALF, "raw_half", 2, nc.scalar)
 
         got_sc = keep.tile([P, S], U8, name="got_sc", align_bytes=64)
         got_w = [keep.tile([P, S], U32, name=f"got_w{a}", align_bytes=64) for a in range(K_PASSES)]
@@ -269,13 +269,23 @@ def tile_list_therapist_pairing_scores_kernel(
             look(b, t)
             larger(b, t)
 
+        warm_in = keep.tile([P, 1], F32, name="warm_in")
+        warm_out = keep.tile([P, 1], F32, name="warm_out")
+        nc.gpsimd.memset(warm_in[:], 0.0)
+        nc.scalar.activation(out=warm_out[:], in_=warm_in[:], func=ACT.Sigmoid)
 
         gather_tab(0)
-        weave_w1(0, 0, 0, "s")
-        weave_w1(0, 0, 1, "s")
+        first = ring.tile([P, PACK, P, PACK], BF16, name="first", tag="woven2", bufs=3, align_bytes=64)
+        for tp in range(2):
+            w1_woven[0, 0, tp] = first[:, 2 * tp : 2 * tp + 2, :, :]
+            weave_w1(0, 0, tp, "s")
         nc.vector.tensor_copy(out=got_sc[:], in_=tab_sc[:].indirect(offs_sb[:]))
-        quant_w1(0, 0, 0)
-        quant_w1(0, 0, 1)
+        first_codes = ring.tile([P, PASS], U32, name="first_codes", tag="tab_sc", align_bytes=64)
+        first_plane = keep.tile([P, PASS], U8, name="first_plane", align_bytes=64)
+        nc.vector.quantize_mx(out=first_codes[:].bitcast(FP8X4), scales=first_plane[:], in_=first[:].rearrange("p t q j -> p (t q j)"))
+        for tp in range(2):
+            w1_codes[0, 0, tp] = first_codes[:, 2 * P * tp : 2 * P * (tp + 1)]
+            w1_planes[0, 0, tp] = first_plane[:, 2 * P * tp : 2 * P * (tp + 1)]
         for t in range(PACK):
             stage1(0, 0, t)
         gather_tab(1)
@@ -301,38 +311,43 @@ def tile_list_therapist_pairing_scores_kernel(
             for t in (2 * tp, 2 * tp + 1):
                 stage1(a, 1, t)
 
-        rows(0, 0, "sv")
-        unit(0, 0, "v")
-        rows(0, 1, "ss")
-        unit(1, 0, "v")
-        rows(0, 2, "ss")
-        unit(2, 0, "v")
-        rows(0, 3, "ss")
-        unit(0, 1, "s")
-        unit(1, 1, "s")
-        unit(2, 1, "s")
+        def finish(b, t):
+            pick(b, t)
+            look(b, t)
+            larger(b, t)
+
+        evac_h(0, 0, "sv")
+        for t in range(PACK):
+            if t + 1 < PACK:
+                evac_h(0, t + 1, "ss")
+            finish(0, t)
+            if t < 3:
+                unit(*divmod(t, 2), "v")
+        for k in range(3, 2 * K_PASSES):
+            unit(*divmod(k, 2), "s")
         weave2("own", 0, 0, M)
         weave2("both", 0, 0, M)
         quant2("own", 0, 0, M)
         quant2("both", 0, 0, M)
+        evac_h(1, 0, "ss")
         for t in range(PACK):
-            rows(1, t, "ss")
+            if t + 1 < PACK:
+                evac_h(1, t + 1, "ss")
+            finish(1, t)
         for m0, width in PARTS:
             stage2("both", 0, m0)
-        for b in range(2):
-            for u in range(2):
-                weave_wc(b, u, "ssss"[2 * b + u])
-        quant_wc(0, 0)
-        quant_wc(0, 1)
+        for u in range(2):
+            weave_wc(0, u, "ss"[u])
+            quant_wc(0, u)
         for m0, width in PARTS:
             stage2("own", 0, m0)
         for k, (m0, width) in enumerate(PARTS):
             weave2("own", 1, m0, width)
-            if k == 0:
-                quant_wc(1, 0)
             weave2("both", 1, m0, width)
             if k == 0:
-                quant_wc(1, 1)
+                for u in range(2):
+                    weave_wc(1, u, "ss"[u])
+                    quant_wc(1, u)
             quant2("own", 1, m0, width)
             stage2("own", 1, m0)
             quant2("both", 1, m0, width)

@@ -182,14 +182,14 @@ def tile_list_therapist_pairing_scores_kernel(
         woven2, codes2, planes2 = {}, {}, {}
 
         def pairs(ap):
-            return ap.rearrange("p t (c i) -> p c t i", i=2)
+            return ap.rearrange("p t (c i) -> p c t i", i=4)
 
         def weave2(kind, b, m0, width):
             cols = slice(m0, m0 + width)
             woven = ring.tile([P, width * PACK], BF16, name="woven2", tag="woven2", bufs=3, align_bytes=64)
-            dst = woven[:].rearrange("p (c i t) -> p c t i", i=2, t=PACK)
+            dst = woven[:].rearrange("p (c i t) -> p c t i", i=4, t=PACK)
             if kind == "own":
-                factor = gain_sb[:, PACK * b : PACK * (b + 1)].unsqueeze(1).unsqueeze(3).broadcast_to([P, width // 2, PACK, 2])
+                factor = gain_sb[:, PACK * b : PACK * (b + 1)].unsqueeze(1).unsqueeze(3).broadcast_to([P, width // 4, PACK, 4])
                 nc.vector.tensor_tensor(out=dst, in0=pairs(own_c[b][:, :, cols]), in1=factor, op=ALU.mult)
             else:
                 nc.vector.tensor_tensor(out=dst, in0=pairs(gate[b][:, :, cols]), in1=pairs(pw[b][:, :, cols]), op=ALU.mult)
@@ -207,7 +207,7 @@ def tile_list_therapist_pairing_scores_kernel(
 
         def weave_wc(b, u, engine):
             woven = ring.tile([P, N_HALF * PACK], BF16, name="wc_woven", tag="wc_woven", bufs=WCB, align_bytes=64)
-            copy_on(engine, woven[:].rearrange("p (c i t) -> p c t i", i=2, t=PACK), pairs(wc_raw[b, u][:]))
+            copy_on(engine, woven[:].rearrange("p (c i t) -> p c t i", i=4, t=PACK), pairs(wc_raw[b, u][:]))
             wc_woven[b, u] = woven
 
         def quant_wc(b, u):
@@ -220,7 +220,7 @@ def tile_list_therapist_pairing_scores_kernel(
         part_banks = {}
         first_bank = 0
         for m0, width in PARTS:
-            per_bank = BANK // width
+            per_bank = min(BANK // width, 3)
             count = -(-6 // per_bank)
             part_banks[m0] = (first_bank, per_bank, width)
             first_bank += count
@@ -311,6 +311,11 @@ def tile_list_therapist_pairing_scores_kernel(
             for t in (2 * tp, 2 * tp + 1):
                 stage1(a, 1, t)
 
+        def unit_rest(a, tp):
+            quant_w1(a, 1, tp)
+            for t in (2 * tp, 2 * tp + 1):
+                stage1(a, 1, t)
+
         def finish(b, t):
             pick(b, t)
             look(b, t)
@@ -320,9 +325,13 @@ def tile_list_therapist_pairing_scores_kernel(
         for t in range(PACK):
             if t + 1 < PACK:
                 evac_h(0, t + 1, "ss")
-            finish(0, t)
+            pick(0, t)
+            look(0, t)
+            if t > 0:
+                unit_rest(*divmod(t - 1, 2))
+            larger(0, t)
             if t < 3:
-                unit(*divmod(t, 2), "v")
+                weave_w1(t // 2, 1, t % 2, "v")
         for k in range(3, 2 * K_PASSES):
             unit(*divmod(k, 2), "s")
         weave2("own", 0, 0, M)
@@ -352,4 +361,4 @@ def tile_list_therapist_pairing_scores_kernel(
             stage2("own", 1, m0)
             quant2("both", 1, m0, width)
             stage2("both", 1, m0)
-            store(m0, "sss" if k < len(PARTS) - 1 else "svs")
+            store(m0, "sss" if k < len(PARTS) - 1 else "sv")

from contextlib import ExitStack

import concourse.mybir as mybir

K, T, S, M, H, N = 1536, 2048, 1024, 512, 1024, 768
FLOPS = 2 * K * H * S + 2 * 2 * H * N * M

F32 = mybir.dt.float32
BF16 = mybir.dt.bfloat16
I32 = mybir.dt.int32
U32 = mybir.dt.uint32
U16 = mybir.dt.uint16
U8 = mybir.dt.uint8
FP8X4 = mybir.dt.float8_e4m3fn_x4
FP4X4 = mybir.dt.float4_e2m1fn_x4
ALU = mybir.AluOpType
ACT = mybir.ActivationFunctionType

P = 128
PACK = 4
PASS = P * PACK
BANK = 512
K_PASSES = K // PASS
H_PASSES = H // PASS
N_HALF = N // 2
M_HALF = M // 2
WCB = 2
PARTS = [(0, 256), (256, 128), (384, 128)]


def tile_list_therapist_pairing_scores_kernel(
    tc, tab_words, tab_scales, offs, pos1, pos2, w1, comfort, reach, pairw, gain, w4_words, w4_scales, wc, out
):
    nc = tc.nc
    with ExitStack() as ctx:
        keep = ctx.enter_context(tc.tile_pool(name="keep", bufs=1))
        ring = ctx.enter_context(tc.tile_pool(name="ring", bufs=1))
        psum = ctx.enter_context(tc.psum_pool(name="psum", bufs=1))

        def copy_on(engine, dst, src):
            if engine == "v":
                nc.vector.tensor_copy(out=dst, in_=src)
            else:
                nc.scalar.copy(out=dst, in_=src)

        offs_sb = keep.tile([P, S // 16], U16, name="offs_sb")
        pos1_sb = keep.tile([P, M // 16], U16, name="pos1_sb")
        pos2_sb = keep.tile([P, M // 16], U16, name="pos2_sb")
        tab_sc = ring.tile([P, T], U8, name="tab_sc", tag="tab_sc", align_bytes=64)
        w4_sc = keep.tile([P, H_PASSES, N], U8, name="w4_sc", align_bytes=64)
        nc.vector.memset(tab_sc[:].bitcast(I32), 0)
        nc.vector.memset(w4_sc[:].rearrange("p a n -> p (a n)").bitcast(I32), 0)

        tab_w = [keep.tile([P, T], I32, name=f"tab_w{a}") for a in range(K_PASSES)]

        def load_tab(a):
            nc.sync.dma_start(out=tab_w[a][:], in_=tab_words[a].rearrange("p t i -> p (t i)").bitcast(I32))

        def load_rows(src, row0, col0, width, tag, bufs, queue=nc.sync):
            raw = ring.tile([P, PACK, width], F32, name=tag, tag=tag, bufs=bufs)
            queue.dma_start(
                out=raw[:], in_=src[row0 : row0 + PASS, col0 : col0 + width].rearrange("(p j) c -> p j c", j=PACK)
            )
            return raw

        def load_vec(src, name):
            vec = keep.tile([P, H_PASSES * PACK], F32, name=name)
            nc.sync.dma_start(
                out=vec[:].rearrange("p (b t) -> p b t", t=PACK), in_=src.rearrange("(b p t) -> p b t", p=P, t=PACK)
            )
            return vec

        w1_raw = {}
        load_tab(0)
        nc.sync.dma_start(offs_sb[:], offs)
        w1_raw[0, 0] = [load_rows(w1, 0, 0, PASS, "raw", 5)]
        tab_sc_i32 = tab_scales.bitcast(I32)
        for q in range(4):
            nc.sync.dma_start(
                out=tab_sc[32 * q : 32 * q + 4 * K_PASSES, :].bitcast(I32), in_=tab_sc_i32[:, 4 * q : 4 * q + 4, :]
            )
        load_tab(1)
        w1_raw[1, 0] = [load_rows(w1, PASS, 0, PASS, "raw", 5)]
        load_tab(2)
        w1_raw[2, 0] = [load_rows(w1, 2 * PASS, u * 256, 256, "raw_half", 2) for u in range(2)]
        nc.sync.dma_start(pos2_sb[:], pos2)
        nc.sync.dma_start(pos1_sb[:], pos1)
        pw, wc_raw = {}, {}
        comfort_sb = load_vec(comfort, "comfort_sb")
        reach_sb = load_vec(reach, "reach_sb")
        w1_raw[0, 1] = [load_rows(w1, 0, PASS, PASS, "raw", 5)]
        w1_raw[1, 1] = [load_rows(w1, PASS, PASS, PASS, "raw", 5)]
        w1_raw[2, 1] = [load_rows(w1, 2 * PASS, PASS, PASS, "raw", 5)]
        gain_sb = load_vec(gain, "gain_sb")
        pw[0] = load_rows(pairw, 0, 0, M, "pw", 2)
        w4 = keep.tile([P, H_PASSES, 2 * N], U8, name="w4", align_bytes=64)
        nc.sync.dma_start(out=w4[:].bitcast(I32), in_=w4_words.bitcast(I32).rearrange("a p x -> p a x"))
        w4_sc_i32 = w4_scales.bitcast(I32)
        for q in range(4):
            nc.sync.dma_start(
                out=w4_sc[32 * q : 32 * q + 4, :, :].bitcast(I32),
                in_=w4_sc_i32[:, 4 * q : 4 * q + 4, :].rearrange("a r n -> r a n"),
            )
        pw[1] = load_rows(pairw, PASS, 0, M, "pw", 2)
        wc_raw[0, 0] = load_rows(wc, 0, 0, N_HALF, "raw_half", 2, nc.scalar)
        wc_raw[0, 1] = load_rows(wc, 0, N_HALF, N_HALF, "raw_half", 2, nc.scalar)
        wc_raw[1, 0] = load_rows(wc, PASS, 0, N_HALF, "raw_half", 2, nc.scalar)
        wc_raw[1, 1] = load_rows(wc, PASS, N_HALF, N_HALF, "raw_half", 2, nc.scalar)

        got_sc = keep.tile([P, S], U8, name="got_sc", align_bytes=64)
        got_w = [keep.tile([P, S], U32, name=f"got_w{a}", align_bytes=64) for a in range(K_PASSES)]

        def gather_tab(a):
            nc.vector.tensor_copy(out=got_w[a][:], in_=tab_w[a][:].bitcast(U32).indirect(offs_sb[:]))

        w1_woven, w1_codes, w1_planes = {}, {}, {}

        def weave_w1(a, b, tp, engine, piece=None):
            if (a, b, tp) not in w1_woven:
                w1_woven[a, b, tp] = ring.tile([P, 2, P, PACK], BF16, name="w1_woven", tag="w1_woven", bufs=4, align_bytes=64)
            woven = w1_woven[a, b, tp]
            raws = w1_raw[a, b]
            nq = P // len(raws)
            for u in range(len(raws)) if piece is None else [piece]:
                src = raws[u][:].rearrange("p j (q t) -> p q j t", t=PACK)[:, :, :, 2 * tp : 2 * tp + 2]
                dst = woven[:, :, u * nq : (u + 1) * nq, :].rearrange("p t q j -> p q j t")
                copy_on(engine, dst, src)

        def quant_w1(a, b, tp):
            codes = keep.tile([P, 2 * P], U32, name=f"w1_codes{a}{b}{tp}", align_bytes=64)
            plane = keep.tile([P, 2 * P], U8, name=f"w1_plane{a}{b}{tp}", align_bytes=64)
            nc.vector.quantize_mx(
                out=codes[:].bitcast(FP8X4), scales=plane[:], in_=w1_woven[a, b, tp][:].rearrange("p t q j -> p (t q j)")
            )
            w1_codes[a, b, tp], w1_planes[a, b, tp] = codes, plane

        h_acc = {}

        def stage1(a, b, t):
            cols = slice((t % 2) * P, (t % 2 + 1) * P)
            for u in range(2):
                if a == 0:
                    h_acc[b, t, u] = psum.tile([P, BANK], F32, name=f"bank{2 * t + u}", tag=f"bank{2 * t + u}")
                tok = slice(u * BANK, (u + 1) * BANK)
                nc.tensor.matmul_mx(
                    out=h_acc[b, t, u][:],
                    lhsT=w1_codes[a, b, t // 2][:, cols].bitcast(FP8X4),
                    lhsT_scale=w1_planes[a, b, t // 2][:, cols],
                    rhs=got_w[a][:, tok].bitcast(FP8X4),
                    rhs_scale=got_sc[4 * a : P, tok],
                    start=(a == 0),
                    stop=(a == K_PASSES - 1),
                )

        h_sb, gate, own_c = {}, {}, {}

        def evac_h(b, t, engines):
            h_sb[b, t] = ring.tile([P, S], F32, name="h_sb", tag="h_sb", bufs=6)
            for u in range(2):
                copy_on(engines[u], h_sb[b, t][:, u * BANK : (u + 1) * BANK], h_acc[b, t, u][:])

        def look(b, t):
            if t == 0:
                gate[b] = ring.tile([P, PACK, M], F32, name="gate", tag="gate", bufs=2)
            col = slice(PACK * b + t, PACK * b + t + 1)
            nc.scalar.activation(
                out=gate[b][:, t, :], in_=h_sb[b, t][:].indirect(pos1_sb[:]), func=ACT.Sigmoid, bias=comfort_sb[:, col]
            )

        def pick(b, t):
            if t == 0:
                own_c[b] = ring.tile([P, PACK, M], F32, name="client", tag="client", bufs=1)
            nc.vector.tensor_copy(out=own_c[b][:, t, :], in_=h_sb[b, t][:].indirect(pos2_sb[:]))

        def larger(b, t):
            col = slice(PACK * b + t, PACK * b + t + 1)
            nc.vector.scalar_tensor_tensor(
                out=gate[b][:, t, :], in0=gate[b][:, t, :], scalar=reach_sb[:, col], in1=own_c[b][:, t, :],
                op0=ALU.mult, op1=ALU.max,
            )

        woven2, codes2, planes2 = {}, {}, {}

        def pairs(ap):
            return ap.rearrange("p t (c i) -> p c t i", i=4)

        def weave2(kind, b, m0, width):
            cols = slice(m0, m0 + width)
            woven = ring.tile([P, width * PACK], BF16, name="woven2", tag="woven2", bufs=3, align_bytes=64)
            dst = woven[:].rearrange("p (c i t) -> p c t i", i=4, t=PACK)
            if kind == "own":
                factor = gain_sb[:, PACK * b : PACK * (b + 1)].unsqueeze(1).unsqueeze(3).broadcast_to([P, width // 4, PACK, 4])
                nc.vector.tensor_tensor(out=dst, in0=pairs(own_c[b][:, :, cols]), in1=factor, op=ALU.mult)
            else:
                nc.vector.tensor_tensor(out=dst, in0=pairs(gate[b][:, :, cols]), in1=pairs(pw[b][:, :, cols]), op=ALU.mult)
            woven2[kind, b, m0] = woven

        def quant2(kind, b, m0, width):
            if (kind, b) not in codes2:
                codes2[kind, b] = {}
            codes = keep.tile([P, width], U32, name=f"{kind}_codes{b}{m0}", align_bytes=64)
            plane = keep.tile([P, width], U8, name=f"{kind}_plane{b}{m0}", align_bytes=64)
            nc.vector.quantize_mx(out=codes[:].bitcast(FP8X4), scales=plane[:], in_=woven2[kind, b, m0][:])
            codes2[kind, b][m0] = (codes, plane, width)

        wc_woven, wc_codes, wc_planes = {}, {}, {}

        def weave_wc(b, u, engine):
            woven = ring.tile([P, N_HALF * PACK], BF16, name="wc_woven", tag="wc_woven", bufs=WCB, align_bytes=64)
            copy_on(engine, woven[:].rearrange("p (c i t) -> p c t i", i=4, t=PACK), pairs(wc_raw[b, u][:]))
            wc_woven[b, u] = woven

        def quant_wc(b, u):
            codes = keep.tile([P, N_HALF], U32, name=f"wc_codes{b}{u}", align_bytes=64)
            plane = keep.tile([P, N_HALF], U8, name=f"wc_plane{b}{u}", align_bytes=64)
            nc.vector.quantize_mx(out=codes[:].bitcast(FP8X4), scales=plane[:], in_=wc_woven[b, u][:])
            wc_codes[b, u], wc_planes[b, u] = codes, plane

        out_acc, seen = {}, {}
        part_banks = {}
        first_bank = 0
        for m0, width in PARTS:
            per_bank = min(BANK // width, 3)
            count = -(-6 // per_bank)
            part_banks[m0] = (first_bank, per_bank, width)
            first_bank += count

        def stage2(kind, b, m0, tiles=range(6)):
            bank0, per_bank, width = part_banks[m0]
            src0 = max(x for x in codes2[kind, b] if x <= m0)
            codes, plane, wide = codes2[kind, b][src0]
            cols = slice(m0 - src0, m0 - src0 + width)
            for nt in tiles:
                bank, side = divmod(nt, per_bank)
                held = min(per_bank, 6 - bank * per_bank)
                if (m0, bank) not in out_acc:
                    out_acc[m0, bank] = psum.tile([P, BANK], F32, name=f"bank{bank0 + bank}", tag=f"bank{bank0 + bank}")
                    seen[m0, bank] = 0
                if kind == "own":
                    u, k = divmod(nt, 3)
                    lhsT = wc_codes[b, u][:, k * P : (k + 1) * P].bitcast(FP8X4)
                    lhsT_scale = wc_planes[b, u][:, k * P : (k + 1) * P]
                else:
                    lhsT = w4[:, b, 2 * nt * P : 2 * (nt + 1) * P].bitcast(FP4X4)
                    lhsT_scale = w4_sc[:, b, nt * P : (nt + 1) * P]
                seen[m0, bank] = seen[m0, bank] + 1
                nc.tensor.matmul_mx(
                    out=out_acc[m0, bank][:, side * width : (side + 1) * width],
                    lhsT=lhsT, lhsT_scale=lhsT_scale,
                    rhs=codes[:, cols].bitcast(FP8X4), rhs_scale=plane[:, cols],
                    start=(seen[m0, bank] == 1), stop=(seen[m0, bank] == 4 * held),
                )

        def store(m0, engines):
            bank0, per_bank, width = part_banks[m0]
            for bank in range(-(-6 // per_bank)):
                held = min(per_bank, 6 - bank * per_bank)
                res = keep.tile([P, held * width], F32, name=f"res{m0}{bank}")
                copy_on(engines[bank], res[:], out_acc[m0, bank][:, : held * width])
                n0 = P * per_bank * bank
                nc.sync.dma_start(
                    out=out[n0 : n0 + held * P, m0 : m0 + width].rearrange("(k p) m -> p k m", p=P),
                    in_=res[:].rearrange("p (k m) -> p k m", k=held),
                )

        def rows(b, t, engines):
            evac_h(b, t, engines)
            pick(b, t)
            look(b, t)
            larger(b, t)

        warm_in = keep.tile([P, 1], F32, name="warm_in")
        warm_out = keep.tile([P, 1], F32, name="warm_out")
        nc.gpsimd.memset(warm_in[:], 0.0)
        nc.scalar.activation(out=warm_out[:], in_=warm_in[:], func=ACT.Sigmoid)

        gather_tab(0)
        first = ring.tile([P, PACK, P, PACK], BF16, name="first", tag="woven2", bufs=3, align_bytes=64)
        for tp in range(2):
            w1_woven[0, 0, tp] = first[:, 2 * tp : 2 * tp + 2, :, :]
            weave_w1(0, 0, tp, "s")
        nc.vector.tensor_copy(out=got_sc[:], in_=tab_sc[:].indirect(offs_sb[:]))
        first_codes = ring.tile([P, PASS], U32, name="first_codes", tag="tab_sc", align_bytes=64)
        first_plane = keep.tile([P, PASS], U8, name="first_plane", align_bytes=64)
        nc.vector.quantize_mx(out=first_codes[:].bitcast(FP8X4), scales=first_plane[:], in_=first[:].rearrange("p t q j -> p (t q j)"))
        for tp in range(2):
            w1_codes[0, 0, tp] = first_codes[:, 2 * P * tp : 2 * P * (tp + 1)]
            w1_planes[0, 0, tp] = first_plane[:, 2 * P * tp : 2 * P * (tp + 1)]
        for t in range(PACK):
            stage1(0, 0, t)
        gather_tab(1)
        weave_w1(1, 0, 0, "s")
        weave_w1(1, 0, 1, "v")
        quant_w1(1, 0, 0)
        quant_w1(1, 0, 1)
        for t in range(PACK):
            stage1(1, 0, t)
        gather_tab(2)
        weave_w1(2, 0, 0, "s", 0)
        weave_w1(2, 0, 0, "v", 1)
        quant_w1(2, 0, 0)
        weave_w1(2, 0, 1, "s", 0)
        weave_w1(2, 0, 1, "s", 1)
        quant_w1(2, 0, 1)
        for t in range(PACK):
            stage1(2, 0, t)

        def unit(a, tp, engine):
            weave_w1(a, 1, tp, engine)
            quant_w1(a, 1, tp)
            for t in (2 * tp, 2 * tp + 1):
                stage1(a, 1, t)

        def unit_rest(a, tp):
            quant_w1(a, 1, tp)
            for t in (2 * tp, 2 * tp + 1):
                stage1(a, 1, t)

        def finish(b, t):
            pick(b, t)
            look(b, t)
            larger(b, t)

        evac_h(0, 0, "sv")
        for t in range(PACK):
            if t + 1 < PACK:
                evac_h(0, t + 1, "ss")
            pick(0, t)
            look(0, t)
            if t > 0:
                unit_rest(*divmod(t - 1, 2))
            larger(0, t)
            if t < 3:
                weave_w1(t // 2, 1, t % 2, "v")
        for k in range(3, 2 * K_PASSES):
            unit(*divmod(k, 2), "s")
        weave2("own", 0, 0, M)
        weave2("both", 0, 0, M)
        quant2("own", 0, 0, M)
        quant2("both", 0, 0, M)
        evac_h(1, 0, "ss")
        for t in range(PACK):
            if t + 1 < PACK:
                evac_h(1, t + 1, "ss")
            finish(1, t)
        for m0, width in PARTS:
            stage2("both", 0, m0)
        for u in range(2):
            weave_wc(0, u, "ss"[u])
            quant_wc(0, u)
        for m0, width in PARTS:
            stage2("own", 0, m0)
        for k, (m0, width) in enumerate(PARTS):
            weave2("own", 1, m0, width)
            weave2("both", 1, m0, width)
            if k == 0:
                for u in range(2):
                    weave_wc(1, u, "ss"[u])
                    quant_wc(1, u)
            quant2("own", 1, m0, width)
            stage2("own", 1, m0)
            quant2("both", 1, m0, width)
            stage2("both", 1, m0)
            store(m0, "sss" if k < len(PARTS) - 1 else "sv")
